import numpy as np
import ml_dtypes


def mxq(x, axis, fmt="e4m3"):
    dtype, down = {"e4m3": (ml_dtypes.float8_e4m3fn, 7), "e5m2": (ml_dtypes.float8_e5m2, 14)}[fmt]
    v = np.moveaxis(np.asarray(x, np.float32).astype(ml_dtypes.bfloat16).astype(np.float64), axis, -1)
    blocks = v.reshape(v.shape[:-1] + (-1, 32))
    amax = np.abs(blocks).max(-1, keepdims=True)
    byte = np.maximum(np.where(amax > 0, np.frexp(amax)[1] - 1 + 127, 0) - down, 1)
    scale = np.exp2(byte - 127.0)
    codes = (blocks / scale).astype(np.float32).astype(dtype).astype(np.float64)
    return np.moveaxis((codes * scale).reshape(v.shape), -1, axis)


WIDE = False


def mx_kscale(k):
    if not WIDE:
        return np.ones(k)
    levels = np.array([30, -30])
    if k % 512:
        return np.exp2(np.random.permutation(np.resize(levels, k // 32))).repeat(32)
    a = np.empty((k // 512, 16))
    for p in range(k // 512):
        a[p, :8] = np.random.permutation(np.resize(levels, 8))
        for g in range(8):
            far = levels[np.abs(levels - a[p, g]) >= 10]
            a[p, g + 8] = far[np.random.randint(len(far))]
    return np.exp2(a.ravel()).repeat(32)


def f64(x):
    return np.asarray(x).astype(np.float64)


def striped(idx):
    return np.tile(np.asarray(idx).reshape(-1, 16).T, (8, 1)).astype(np.uint16)


def unstriped(offs):
    return offs[:16].T.reshape(-1).astype(np.int64)


def striped8(idx):
    return np.asarray(idx).reshape(8, -1, 16).transpose(0, 2, 1).reshape(128, -1).astype(np.uint16)


def unstriped8(offs):
    return offs.reshape(8, 16, -1).transpose(0, 2, 1).reshape(8, -1).astype(np.int64)


def pick8(x, idx, run):
    r = np.arange(len(x))
    return x[r[:, None], idx[r % (8 * run) // run]]


E2M1 = np.array([0.0, 0.5, 1.0, 1.5, 2.0, 3.0, 4.0, 6.0, -0.0, -0.5, -1.0, -1.5, -2.0, -3.0, -4.0, -6.0])


def pack_weight(w, fmt):
    k, n = w.shape
    w = f64(np.asarray(w, np.float32).astype(ml_dtypes.bfloat16)).reshape(k // 32, 32, n)
    amax = np.abs(w).max(1)
    if fmt in ("e4m3", "e5m2"):
        byte = np.frexp(amax)[1] - 1 + 127 - (7 if fmt == "e4m3" else 14)
    else:
        mant, ex = np.frexp(amax / 6.0)
        byte = np.where(mant > 0.5, ex, ex - 1) + 127
    byte = np.clip(np.where(amax > 0, byte, 1), 1, 254)
    scaled = (w * np.exp2(127.0 - byte)[:, None, :]).reshape(k, n).astype(np.float32)
    by_word = np.ascontiguousarray(scaled.reshape(k // 512, 128, 4, n).transpose(0, 1, 3, 2))
    if fmt in ("e4m3", "e5m2"):
        words = by_word.astype(ml_dtypes.float8_e4m3fn if fmt == "e4m3" else ml_dtypes.float8_e5m2).view(np.uint8)
    else:
        c = by_word.astype(ml_dtypes.float4_e2m1fn).view(np.uint8) & 0xF
        words = (c[..., 0::2] | (c[..., 1::2] << 4)).reshape(k // 512, 128, 2 * n)
    return np.ascontiguousarray(words), np.ascontiguousarray(byte.astype(np.uint8).reshape(k // 512, 16, n))


def unpack_weight(words, scales, fmt):
    g, _, n = scales.shape
    words = np.ascontiguousarray(words).reshape(g, 128, n, -1)
    if fmt in ("e4m3", "e5m2"):
        vals = words.view(ml_dtypes.float8_e4m3fn if fmt == "e4m3" else ml_dtypes.float8_e5m2).astype(np.float64)
    else:
        nib = np.empty((g, 128, n, 4), np.uint8)
        nib[..., 0::2] = words & 0xF
        nib[..., 1::2] = words >> 4
        vals = E2M1[nib]
    vals = vals * np.repeat(np.exp2(scales.astype(np.float64) - 127.0), 8, axis=1)[..., None]
    return vals.transpose(0, 1, 3, 2).reshape(g * 512, n)


K, T, J, R, F, Z, N, C, O = 512, 1024, 256, 512, 512, 1024, 256, 512, 128


def setup_inputs():
    n = np.random.standard_normal
    idx = np.random.permutation(T)[:J]
    idx2 = np.random.permutation(Z)[:J]
    idx3 = np.stack([np.random.permutation(C)[:J] for _ in range(8)])
    idx4 = np.random.permutation(C)[:O]
    idx5 = np.random.permutation(J)[:O]
    ff = mx_kscale(F)
    fk = mx_kscale(K)
    fr = mx_kscale(R)
    xop = pack_weight(n((F, Z)) / ff[:, None], "e5m2")
    wp = pack_weight(n((K, R)) * 1 / np.sqrt(K) / fk[:, None] * fr, "e5m2")
    w2p = pack_weight(n((F, R)) * 1 / np.sqrt(F) * ff[:, None] * fr, "e4m3")
    wbp = pack_weight(n((R, N)) * 1 / np.sqrt(R) / fr[:, None], "e4m3")
    wcp = pack_weight(n((R, N)) * 1 / np.sqrt(R) / fr[:, None], "e2m1")
    return {
        "xo_words": xop[0],
        "xo_scales": xop[1],
        "cq": (np.random.randint(-7, 8, (K, T)).astype(np.float64)).astype(np.float32),
        "gs": (np.random.uniform(0.1, 0.4, (K, 1)) * fk[:, None]).astype(np.float32),
        "w_words": wp[0],
        "w_scales": wp[1],
        "w2_words": w2p[0],
        "w2_scales": w2p[1],
        "wb_words": wbp[0],
        "wb_scales": wbp[1],
        "wc_words": wcp[0],
        "wc_scales": wcp[1],
        "so": (np.random.uniform(0.5, 1.6, (N, 1))).astype(np.float32),
        "sp": (np.random.uniform(0.5, 1.6, (N, 1))).astype(np.float32),
        "offs": striped(idx),
        "offs2": striped(idx2),
        "offs3": striped8(idx3),
        "offs4": striped(idx4),
        "offs5": striped(idx5),
    }


def reference(xo_words, xo_scales, cq, gs, w_words, w_scales, w2_words, w2_scales, wb_words, wb_scales, wc_words, wc_scales, so, sp, offs, offs2, offs3, offs4, offs5):
    idx = unstriped(offs)
    idx2 = unstriped(offs2)
    idx3 = unstriped8(offs3)
    idx4 = unstriped(offs4)
    idx5 = unstriped(offs5)
    xou = unpack_weight(xo_words, xo_scales, "e5m2")
    wu = unpack_weight(w_words, w_scales, "e5m2")
    w2u = unpack_weight(w2_words, w2_scales, "e4m3")
    wbu = unpack_weight(wb_words, wb_scales, "e4m3")
    wcu = unpack_weight(wc_words, wc_scales, "e2m1")
    x1 = f64(cq)[:, idx] * f64(gs)
    x1q = mxq(x1, 0, "e4m3")
    a = wu.T @ x1q
    xoidx2g = xou[:, idx2]
    b = w2u.T @ xoidx2g
    hid = np.maximum(a, b)
    hidq = mxq(hid, 0, "e5m2")
    p = wbu.T @ hidq
    q = wcu.T @ hidq
    pw = np.zeros((N, C))
    pw[np.arange(N)[:, None], idx3[np.arange(N) % 128 // 16]] = p
    y = pw[:, idx4] * f64(so) - q[:, idx5] * f64(sp)
    return y

from contextlib import ExitStack

import concourse.mybir as mybir

K, T, J, R, F, Z, N, C, O = 512, 1024, 256, 512, 512, 1024, 256, 512, 128
FLOPS = 2 * J * (K * R + F * R + 2 * R * N)

F32 = mybir.dt.float32
BF16 = mybir.dt.bfloat16
I32 = mybir.dt.int32
U32 = mybir.dt.uint32
U16 = mybir.dt.uint16
U8 = mybir.dt.uint8
E4M3 = mybir.dt.float8_e4m3fn_x4
E5M2 = mybir.dt.float8_e5m2_x4
E2M1 = mybir.dt.float4_e2m1fn_x4
COPY = mybir.ActivationFunctionType.Copy
ALU = mybir.AluOpType

P = 128
PACK = 4
QUADS = 4
QUAD = 32
HALF = 128
HALVES = J // HALF
LIST_COLS = HALF // 16
N_TILES = N // P


def tile_list_outcomeownboard_codednote_kernel(
    tc, xo_words, xo_scales, cq, gs, w_words, w_scales, w2_words, w2_scales, wb_words, wb_scales,
    wc_words, wc_scales, so, sp, offs, offs2, offs3, offs4, offs5, out,
):
    nc = tc.nc
    with ExitStack() as ctx:
        sb = ctx.enter_context(tc.tile_pool(name="sb", bufs=1))
        ps = ctx.enter_context(tc.psum_pool(name="ps", bufs=1))

        def tile(name, shape, dtype, tag=None):
            return sb.tile(shape, dtype, name=name, tag=tag or name, align_bytes=64)

        def words(ap):
            return ap[0].rearrange("p c b -> p (c b)").bitcast(I32)

        def scale_rows(ap):
            return ap[0].bitcast(I32).rearrange("(q r) c -> r q c", r=PACK)

        idx = tile("idx", [P, J // 16], U16)
        idx2 = tile("idx2", [P, J // 16], U16)
        idx3 = tile("idx3", [P, J // 16], U16)
        idx4 = tile("idx4", [P, O // 16], U16)
        idx5 = tile("idx5", [P, O // 16], U16)
        cq_sb = [tile("cq%d" % i, [P, T], F32) for i in range(PACK)]
        gs_sb = tile("gs", [P, PACK], F32)
        w_raw = tile("w_raw", [P, R], U32)
        w2_raw = tile("w2_raw", [P, R], U32)
        xo_sb = tile("xo", [P, Z], U32)
        wb_sb = tile("wb", [P, N], U32)
        wc_sb = tile("wc", [P, 2 * N], U8)
        cq_rows = cq.rearrange("(p i) t -> i p t", i=PACK)
        nc.sync.dma_start(cq_sb[0][:], cq_rows[0])
        nc.sync.dma_start(idx[:], offs)
        nc.sync.dma_start(gs_sb[:], gs.rearrange("(p i) o -> p (i o)", i=PACK))
        low_stage = tile("low_stage", [PACK, QUADS, (2 * R + 2 * N) // 4], I32)
        xo_stage = tile("xo_stage", [P, 2, Z // 4], I32)
        HIGH = 64
        nc.sync.dma_start(low_stage[:, :, 0 : R // 4], scale_rows(w_scales))
        nc.sync.dma_start(low_stage[:, :, R // 4 : 2 * R // 4], scale_rows(w2_scales))
        for s in range(2):
            nc.sync.dma_start(xo_stage[HIGH * s : HIGH * s + PACK], scale_rows(xo_scales)[:, 2 * s : 2 * s + 2, :])
        nc.sync.dma_start(cq_sb[1][:], cq_rows[1])
        nc.sync.dma_start(cq_sb[2][:], cq_rows[2])
        nc.sync.dma_start(low_stage[:, :, 2 * R // 4 : (2 * R + N) // 4], scale_rows(wb_scales))
        nc.sync.dma_start(low_stage[:, :, (2 * R + N) // 4 :], scale_rows(wc_scales))
        nc.sync.dma_start(idx2[:], offs2)
        nc.sync.dma_start(cq_sb[3][:], cq_rows[3])
        nc.sync.dma_start(w_raw[:].bitcast(I32), words(w_words))
        nc.sync.dma_start(w2_raw[:].bitcast(I32), words(w2_words))
        nc.sync.dma_start(xo_sb[:].bitcast(I32), words(xo_words))
        nc.sync.dma_start(wb_sb[:].bitcast(I32), words(wb_words))
        nc.sync.dma_start(wc_sb[:].bitcast(I32), wc_words[0].bitcast(I32))
        nc.sync.dma_start(idx3[:], offs3)
        so_sb = tile("so", [P, N_TILES], F32)
        sp_sb = tile("sp", [P, N_TILES], F32)
        with nc.allow_non_contiguous_dma(reason="one weight a partition"):
            nc.sync.dma_start(so_sb[:], so.rearrange("(u p) o -> p (u o)", p=P))
            nc.sync.dma_start(sp_sb[:], sp.rearrange("(u p) o -> p (u o)", p=P))
        nc.sync.dma_start(idx4[:], offs4)
        nc.sync.dma_start(idx5[:], offs5)

        w_plane = tile("w_plane", [P, 2 * R], U8)
        late_plane = tile("late_plane", [P, 2 * N], U8)
        xo_plane = tile("xo_plane", [P, Z], U8)
        for plane in (w_plane, xo_plane, late_plane):
            nc.vector.memset(plane[:].bitcast(I32), 0)

        board = [tile("board%d" % u, [P, C], F32) for u in range(N_TILES)]
        for u in range(N_TILES):
            nc.vector.memset(board[u][:], 0.0)

        for q in range(QUADS):
            nc.vector.tensor_copy(w_plane[QUAD * q : QUAD * q + PACK, :].bitcast(I32), low_stage[:, q, 0 : 2 * R // 4])
        dealt_plane = tile("dealt_plane", [P, 2, PACK, P], U8)
        nc.vector.tensor_copy(
            dealt_plane[:].rearrange("p w t m -> p w m t"),
            w_plane[:].rearrange("p (w m t) -> p w m t", w=2, t=PACK),
        )
        for q in range(QUADS):
            start = HIGH * (q // 2)
            nc.vector.tensor_copy(xo_plane[QUAD * q : QUAD * q + PACK, :].bitcast(I32), xo_stage[start : start + PACK, q % 2, :])
        xo_picked_plane = tile("xo_picked_plane", [P, J], U8)
        for q in range(QUADS):
            nc.vector.tensor_copy(late_plane[QUAD * q : QUAD * q + PACK, :].bitcast(I32), low_stage[:, q, 2 * R // 4 :])
        wb_plane = late_plane[:, 0:N]
        wc_plane = late_plane[:, N:]

        x1_rows = tile("x1_rows", [P, PACK, J], BF16)
        for i in range(PACK):
            nc.scalar.activation(x1_rows[:, i, :], cq_sb[i][:].indirect(idx[:]), COPY, scale=gs_sb[:, i : i + 1])
        nc.vector.tensor_copy(xo_picked_plane[:], xo_plane[:].indirect(idx2[:]))

        w_dealt = tile("w_dealt", [P, PACK, P], U32)
        w2_dealt = tile("w2_dealt", [P, PACK, P], U32)
        nc.scalar.copy(w_dealt[:].rearrange("p t m -> p m t"), w_raw[:].rearrange("p (m t) -> p m t", t=PACK))

        x1_woven = [tile("x1_woven%d" % h, [P, HALF, PACK], BF16) for h in range(HALVES)]
        x1_codes = [tile("x1_codes%d" % h, [P, HALF], U32) for h in range(HALVES)]
        x1_plane = [tile("x1_plane%d" % h, [P, HALF], U8) for h in range(HALVES)]
        for h in range(HALVES):
            nc.vector.tensor_copy(
                x1_woven[h][:].rearrange("p (c e) i -> p c i e", e=4),
                x1_rows[:, :, HALF * h : HALF * (h + 1)].rearrange("p i (c e) -> p c i e", e=4),
            )
        for h in range(HALVES):
            nc.vector.quantize_mx(x1_codes[h][:].bitcast(E4M3), x1_plane[h][:], x1_woven[h][:].rearrange("p j i -> p (j i)"))

        nc.vector.tensor_copy(w2_dealt[:].bitcast(I32).rearrange("p t m -> p m t"),
                              w2_raw[:].bitcast(I32).rearrange("p (m t) -> p m t", t=PACK))
        xo_picked = [tile("xo_picked%d" % h, [P, HALF], U32, tag="x1_woven%d" % h) for h in range(HALVES)]
        for h in range(HALVES):
            nc.vector.tensor_copy(xo_picked[h][:], xo_sb[:].indirect(idx2[:, LIST_COLS * h : LIST_COLS * (h + 1)]))

        a_sb = []
        b_ps = []
        for h in range(HALVES):
            a_ps = ps.tile([P, PACK, HALF], F32, name="a_ps%d" % h)
            for t in range(PACK):
                nc.tensor.matmul_mx(a_ps[:, t, :], w_dealt[:, t, :].bitcast(E5M2), dealt_plane[:, 0, t, :],
                                    x1_codes[h][:].bitcast(E4M3), x1_plane[h][:], start=True, stop=True)
            a_sb.append(tile("a_sb%d" % h, [P, HALF, PACK], F32))
            nc.scalar.copy(a_sb[h][:], a_ps[:].rearrange("p t j -> p j t"))
            b_ps.append(ps.tile([P, PACK, HALF], F32, name="b_ps%d" % h))
            for t in range(PACK):
                nc.tensor.matmul_mx(b_ps[h][:, t, :], w2_dealt[:, t, :].bitcast(E4M3), dealt_plane[:, 1, t, :],
                                    xo_picked[h][:].bitcast(E5M2), xo_picked_plane[:, HALF * h : HALF * (h + 1)],
                                    start=True, stop=True)

        hid_codes = tile("hid_codes", [P, J], U32)
        hid_plane = tile("hid_plane", [P, J], U8)
        PIECE = HALF // 2
        p_sb = {}
        for h in range(HALVES):
            pieces = [slice(PIECE * s, PIECE * (s + 1)) for s in range(2)]
            hid = [tile("hid%d%d" % (h, s), [P, PIECE, PACK], BF16, tag="hid%d" % ((s + h) % 2)) for s in range(2)]
            for s, piece in enumerate(pieces):
                nc.vector.tensor_tensor(hid[s][:], b_ps[h][:, :, piece].rearrange("p t j -> p j t"),
                                        a_sb[h][:, piece, :], ALU.max)
            for s, piece in enumerate(pieces):
                cols = slice(HALF * h + piece.start, HALF * h + piece.stop)
                nc.vector.quantize_mx(hid_codes[:, cols].bitcast(E5M2), hid_plane[:, cols],
                                      hid[s][:].rearrange("p j t -> p (j t)"))
            cols = slice(HALF * h, HALF * (h + 1))
            for u in range(N_TILES):
                rows = slice(P * u, P * (u + 1))
                p_ps = ps.tile([P, HALF], F32, name="p_ps%d" % u)
                nc.tensor.matmul_mx(p_ps[:], wb_sb[:, rows].bitcast(E4M3), wb_plane[:, rows],
                                    hid_codes[:, cols].bitcast(E5M2), hid_plane[:, cols], start=True, stop=True)
                p_sb[h, u] = tile("p_sb%d%d" % (h, u), [P, HALF], F32)
                if (h, u) == (0, 0):
                    nc.scalar.copy(p_sb[h, u][:], p_ps[:])
                else:
                    nc.vector.tensor_copy(p_sb[h, u][:], p_ps[:])
                nc.scalar.activation(board[u][:].indirect(idx3[:, LIST_COLS * h : LIST_COLS * (h + 1)]), p_sb[h, u][:], COPY)

        for u in range(N_TILES):
            q_ps = ps.tile([P, J], F32, name="q_ps%d" % u)
            nc.tensor.matmul_mx(q_ps[:], wc_sb[:, 2 * P * u : 2 * P * (u + 1)].bitcast(E2M1), wc_plane[:, P * u : P * (u + 1)],
                                hid_codes[:].bitcast(E5M2), hid_plane[:], start=True, stop=True)
            q_sb = tile("q_sb%d" % u, [P, J], F32)
            nc.vector.tensor_copy(q_sb[:], q_ps[:])
            taken = tile("taken%d" % u, [P, O], F32)
            nc.scalar.activation(taken[:], q_sb[:].indirect(idx5[:]), COPY, scale=sp_sb[:, u : u + 1])
            kept = tile("kept%d" % u, [P, O], F32)
            nc.scalar.activation(kept[:], board[u][:].indirect(idx4[:]), COPY, scale=so_sb[:, u : u + 1])
            result = tile("result%d" % u, [P, O], F32)
            nc.vector.tensor_tensor(result[:], kept[:], taken[:], ALU.subtract)
            nc.sync.dma_start(out[P * u : P * (u + 1), :], result[:])
